import numpy as np
import ml_dtypes


def mxq(x, axis, fmt="e4m3"):
    dtype, down = {"e4m3": (ml_dtypes.float8_e4m3fn, 7), "e5m2": (ml_dtypes.float8_e5m2, 14)}[fmt]
    v = np.moveaxis(np.asarray(x, np.float32).astype(ml_dtypes.bfloat16).astype(np.float64), axis, -1)
    blocks = v.reshape(v.shape[:-1] + (-1, 32))
    amax = np.abs(blocks).max(-1, keepdims=True)
    byte = np.maximum(np.where(amax > 0, np.frexp(amax)[1] - 1 + 127, 0) - down, 1)
    scale = np.exp2(byte - 127.0)
    codes = (blocks / scale).astype(np.float32).astype(dtype).astype(np.float64)
    return np.moveaxis((codes * scale).reshape(v.shape), -1, axis)


WIDE = False


def mx_kscale(k):
    if not WIDE:
        return np.ones(k)
    levels = np.array([10, -10, 5, -5, 0])
    if k % 512:
        return np.exp2(np.random.permutation(np.resize(levels, k // 32))).repeat(32)
    a = np.empty((k // 512, 16))
    for p in range(k // 512):
        a[p, :8] = np.random.permutation(np.resize(levels, 8))
        for g in range(8):
            far = levels[np.abs(levels - a[p, g]) >= 10]
            a[p, g + 8] = far[np.random.randint(len(far))]
    return np.exp2(a.ravel()).repeat(32)


def f64(x):
    return np.asarray(x).astype(np.float64)


def striped8(idx):
    return np.asarray(idx).reshape(8, -1, 16).transpose(0, 2, 1).reshape(128, -1).astype(np.uint16)


def unstriped8(offs):
    return offs.reshape(8, 16, -1).transpose(0, 2, 1).reshape(8, -1).astype(np.int64)


def pick8(x, idx, run):
    r = np.arange(len(x))
    return x[r[:, None], idx[r % (8 * run) // run]]


E2M1 = np.array([0.0, 0.5, 1.0, 1.5, 2.0, 3.0, 4.0, 6.0, -0.0, -0.5, -1.0, -1.5, -2.0, -3.0, -4.0, -6.0])


def pack_weight(w, fmt):
    k, n = w.shape
    w = f64(np.asarray(w, np.float32).astype(ml_dtypes.bfloat16)).reshape(k // 32, 32, n)
    amax = np.abs(w).max(1)
    if fmt == "e4m3":
        byte = np.frexp(amax)[1] - 1 + 127 - 7
    else:
        mant, ex = np.frexp(amax / 6.0)
        byte = np.where(mant > 0.5, ex, ex - 1) + 127
    byte = np.clip(np.where(amax > 0, byte, 1), 1, 254)
    scaled = (w * np.exp2(127.0 - byte)[:, None, :]).reshape(k, n).astype(np.float32)
    by_word = np.ascontiguousarray(scaled.reshape(k // 512, 128, 4, n).transpose(0, 1, 3, 2))
    if fmt == "e4m3":
        words = by_word.astype(ml_dtypes.float8_e4m3fn).view(np.uint8)
    else:
        c = by_word.astype(ml_dtypes.float4_e2m1fn).view(np.uint8) & 0xF
        words = (c[..., 0::2] | (c[..., 1::2] << 4)).reshape(k // 512, 128, 2 * n)
    return np.ascontiguousarray(words), np.ascontiguousarray(byte.astype(np.uint8).reshape(k // 512, 16, n))


def unpack_weight(words, scales, fmt):
    g, _, n = scales.shape
    words = np.ascontiguousarray(words).reshape(g, 128, n, -1)
    if fmt == "e4m3":
        vals = words.view(ml_dtypes.float8_e4m3fn).astype(np.float64)
    else:
        nib = np.empty((g, 128, n, 4), np.uint8)
        nib[..., 0::2] = words & 0xF
        nib[..., 1::2] = words >> 4
        vals = E2M1[nib]
    vals = vals * np.repeat(np.exp2(scales.astype(np.float64) - 127.0), 8, axis=1)[..., None]
    return vals.transpose(0, 1, 3, 2).reshape(g * 512, n)


def softplus(v):
    return np.log(1.0 + np.exp(v))


D, T, I, Q = 512, 1024, 512, 128


def setup_inputs():
    n = np.random.standard_normal
    idx = np.stack([np.random.permutation(T)[:I] for _ in range(8)])
    fd = mx_kscale(D)
    keysp = pack_weight(n((D, T)) / fd[:, None], "e2m1")
    return {
        "query": (n((D, Q)) * 0.9 / np.sqrt(D) * fd[:, None]).astype(np.float32),
        "query2": (n((D, Q)) * 0.9 / np.sqrt(D) * fd[:, None]).astype(np.float32),
        "keys_words": keysp[0],
        "keys_scales": keysp[1],
        "lam": (np.random.uniform(1.0, 2.0, (Q, 1))).astype(np.float32),
        "old": (np.random.uniform(0.0, 2.0, (Q, T))).astype(np.float32),
        "fade": (np.random.uniform(0.3, 0.9, (Q, 1))).astype(np.float32),
        "offs": striped8(idx),
    }


def reference(query, query2, keys_words, keys_scales, lam, old, fade, offs):
    idx = unstriped8(offs)
    keysu = unpack_weight(keys_words, keys_scales, "e2m1")
    queryq = mxq(f64(query), 0, "e4m3")
    a = queryq.T @ keysu
    query2q = mxq(f64(query2), 0, "e4m3")
    b = query2q.T @ keysu
    ra = np.sqrt(softplus(pick8(a, idx, 16)) * softplus(pick8(b, idx, 16)) + 0.1)
    s = ra * f64(lam) - np.abs(pick8(a, idx, 16) - pick8(b, idx, 16))
    p = np.exp(s - np.max(s, axis=1, keepdims=True))
    w = p / np.sum(p, axis=1, keepdims=True)
    ws = w * 256.0
    wf = np.zeros((Q, T))
    wf[np.arange(Q)[:, None], idx[np.arange(Q) % 128 // 16]] = ws
    y = f64(old) * f64(fade) + wf
    return y

@@ -1,0 +1,163 @@
+import math
+from contextlib import ExitStack
+
+import concourse.mybir as mybir
+
+F32 = mybir.dt.float32
+BF16 = mybir.dt.bfloat16
+I32 = mybir.dt.int32
+U32 = mybir.dt.uint32
+U16 = mybir.dt.uint16
+U8 = mybir.dt.uint8
+FP8X4 = mybir.dt.float8_e4m3fn_x4
+FP4X4 = mybir.dt.float4_e2m1fn_x4
+ALU = mybir.AluOpType
+ACT = mybir.ActivationFunctionType
+AX = mybir.AxisListType
+
+D, T, I, Q = 512, 1024, 512, 128
+P = 128
+PACK = 4
+N = 512
+FLOPS = 2 * 2 * D * Q * T
+
+EXP_CAP = 2.0**60
+SP_CAP = math.log(1.0 + EXP_CAP)
+PIECE = 256
+STORE_WIDTHS = [256, 256, 256, 256]
+ROOT_WIDTHS = [256, 256]
+PICK_WIDTHS = [256, 256]
+
+
+def spans(widths):
+    edges = [sum(widths[:j]) for j in range(len(widths) + 1)]
+    return [slice(edges[j], edges[j + 1]) for j in range(len(widths))]
+
+
+def tile_attend_agreeingtwo_soft_counts_heads_kernel(tc, query, query2, keys_words, keys_scales, lam, old, fade, offs, out):
+    nc = tc.nc
+    with ExitStack() as ctx:
+        sb = ctx.enter_context(tc.tile_pool(name="sb", bufs=1))
+        ps = ctx.enter_context(tc.psum_pool(name="ps", bufs=1))
+
+        offsets = sb.tile([P, I // 16], U16, name="offsets")
+        plane = sb.tile([P, T], U8, name="plane", align_bytes=64)
+        words = [sb.tile([P, T], U8, name=f"words{h}", align_bytes=64) for h in range(2)]
+        wf = sb.tile([P, T], F32, name="wf")
+        old_sb = sb.tile([P, T], F32, name="old_sb")
+        lam_sb = sb.tile([P, 1], F32, name="lam_sb")
+        fade_sb = sb.tile([P, 1], F32, name="fade_sb")
+        raw = [sb.tile([P, PACK, Q], F32, name=f"raw{j}") for j in range(2)]
+        grouped = [sb.tile([P, Q, PACK], BF16, name=f"grouped{j}", align_bytes=64) for j in range(2)]
+        codes = [sb.tile([P, Q], U32, name=f"codes{j}", align_bytes=64) for j in range(2)]
+        qscale = [sb.tile([P, Q], U8, name=f"qscale{j}", align_bytes=64) for j in range(2)]
+        score = [sb.tile([P, T], F32, name=f"score{j}") for j in range(2)]
+        pieces = T // PIECE
+        banks = [[ps.tile([P, PIECE], F32, name=f"bank{j}_{h}") for h in range(pieces)] for j in range(2)]
+
+        nc.vector.memset(plane[:].bitcast(U32), 0)
+        nc.sync.dma_start(out=raw[0][:], in_=query.rearrange("(p j) w -> p j w", j=PACK))
+        for quad in range(4):
+            nc.scalar.dma_start(
+                out=plane[32 * quad : 32 * quad + 4, :].bitcast(I32),
+                in_=keys_scales[0, 4 * quad : 4 * quad + 4, :].bitcast(I32),
+            )
+        nc.sync.dma_start(out=raw[1][:], in_=query2.rearrange("(p j) w -> p j w", j=PACK))
+        for h in range(2):
+            nc.sync.dma_start(out=words[h][:].bitcast(I32), in_=keys_words[0, :, T * h : T * (h + 1)].bitcast(I32))
+        nc.sync.dma_start(offsets[:], offs)
+        nc.sync.dma_start(out=old_sb[:], in_=old)
+        nc.sync.dma_start(out=lam_sb[:], in_=lam)
+        nc.sync.dma_start(out=fade_sb[:], in_=fade)
+        nc.vector.memset(wf[:], 0.0)
+
+        def interleaved(j):
+            dst = grouped[j][:].rearrange("p (c i) t -> p c t i", i=4)
+            src = raw[j][:].rearrange("p t (c i) -> p c t i", i=4)
+            return dst, src
+
+        def quantize(j):
+            nc.vector.quantize_mx(
+                out=codes[j][:].bitcast(FP8X4), scales=qscale[j][:], in_=grouped[j][:].rearrange("p w t -> p (w t)")
+            )
+
+        dst, src = interleaved(0)
+        nc.vector.tensor_copy(out=dst, in_=src)
+        quantize(0)
+        dst, src = interleaved(1)
+        nc.scalar.activation(dst, src, ACT.Copy)
+        quantize(1)
+
+        for j in range(2):
+            for h in range(pieces):
+                byte0 = 2 * PIECE * h % T
+                nc.tensor.matmul_mx(
+                    out=banks[j][h][:],
+                    lhsT=codes[j][:].bitcast(FP8X4),
+                    lhsT_scale=qscale[j][:],
+                    rhs=words[2 * PIECE * h // T][:, byte0 : byte0 + 2 * PIECE].bitcast(FP4X4),
+                    rhs_scale=plane[:, PIECE * h : PIECE * (h + 1)],
+                    start=True,
+                    stop=True,
+                )
+        for j in range(2):
+            for h in range(pieces):
+                cols = slice(PIECE * h, PIECE * (h + 1))
+                if j == 0 and h % 2 == 1:
+                    nc.vector.tensor_copy(out=score[j][:, cols], in_=banks[j][h][:])
+                else:
+                    nc.scalar.activation(score[j][:, cols], banks[j][h][:], ACT.Copy)
+
+        ex = [sb.tile([P, I], F32, name=f"ex{j}") for j in range(2)]
+        picked = [sb.tile([P, I], F32, name=f"picked{j}") for j in range(2)]
+        soft = [sb.tile([P, I], F32, name=f"soft{j}") for j in range(2)]
+        nc.vector.tensor_copy(out=picked[0][:], in_=score[0][:].indirect(offsets[:]))
+        nc.scalar.activation(ex[0][:], picked[0][:], ACT.Exp)
+        for cols in spans(PICK_WIDTHS):
+            nc.vector.tensor_copy(
+                out=picked[1][:, cols], in_=score[1][:].indirect(offsets[:, cols.start // 16 : cols.stop // 16])
+            )
+            nc.scalar.activation(ex[1][:, cols], picked[1][:, cols], ACT.Exp)
+        over_b = sb.tile([P, I], F32, name="over_b")
+        over = sb.tile([P, I], F32, name="over")
+        nc.vector.tensor_scalar_min(ex[0][:], ex[0][:], EXP_CAP)
+        nc.vector.tensor_scalar(over_b[:], picked[1][:], SP_CAP, 1.0 / (SP_CAP * SP_CAP), ALU.max, ALU.mult)
+        nc.vector.tensor_scalar_min(ex[1][:], ex[1][:], EXP_CAP)
+        nc.vector.scalar_tensor_tensor(over[:], picked[0][:], SP_CAP, over_b[:], ALU.max, ALU.mult)
+
+        part = sb.tile([P, I], F32, name="part")
+        prod = sb.tile([P, I], F32, name="prod")
+        logu = sb.tile([P, I], F32, name="logu")
+        root = sb.tile([P, I], F32, name="root")
+        diff = sb.tile([P, I], F32, name="diff")
+        negabs = sb.tile([P, I], F32, name="negabs")
+        s = sb.tile([P, I], F32, name="s")
+        p = sb.tile([P, I], F32, name="p")
+        ws = sb.tile([P, I], F32, name="ws")
+        negmax = sb.tile([P, 1], F32, name="negmax")
+        total = sb.tile([P, 1], F32, name="total")
+        inv = sb.tile([P, 1], F32, name="inv")
+        halves = spans([I // 2, I // 2])
+        for cols in halves:
+            nc.scalar.activation(soft[0][:, cols], ex[0][:, cols], ACT.Ln, bias=1.0)
+            nc.vector.tensor_tensor(part[:, cols], soft[0][:, cols], over[:, cols], ALU.mult)
+        for cols in halves:
+            nc.scalar.activation(soft[1][:, cols], ex[1][:, cols], ACT.Ln, bias=1.0)
+            nc.vector.tensor_tensor(prod[:, cols], part[:, cols], soft[1][:, cols], ALU.mult)
+        for cols in halves:
+            nc.scalar.activation(logu[:, cols], prod[:, cols], ACT.Ln, bias=0.1)
+        nc.vector.tensor_tensor(diff[:], picked[0][:], picked[1][:], ALU.subtract)
+        nc.vector.scalar_tensor_tensor(negabs[:], diff[:], -1.0, diff[:], ALU.mult, ALU.min)
+        for cols in spans(ROOT_WIDTHS):
+            nc.scalar.activation(root[:, cols], logu[:, cols], ACT.Exp, scale=0.5)
+            nc.vector.scalar_tensor_tensor(s[:, cols], root[:, cols], lam_sb[:], negabs[:, cols], ALU.mult, ALU.add)
+        nc.vector.tensor_reduce(negmax[:], s[:], AX.X, ALU.max, negate=True)
+        nc.scalar.activation(p[:], s[:], ACT.Exp, bias=negmax[:], accum_out=total[:])
+        nc.vector.reciprocal(inv[:], total[:])
+        nc.vector.tensor_scalar(ws[:], p[:], inv[:], 256.0, ALU.mult, ALU.mult)
+        nc.vector.tensor_copy(out=wf[:].indirect(offsets[:]), in_=ws[:])
+
+        for c, cols in enumerate(spans(STORE_WIDTHS)):
+            res = sb.tile([P, STORE_WIDTHS[c]], F32, name=f"res{c}")
+            nc.vector.scalar_tensor_tensor(res[:], old_sb[:, cols], fade_sb[:], wf[:, cols], ALU.mult, ALU.add)
+            nc.sync.dma_start(out=out[:, cols], in_=res[:])

@@ -1,4 +1,3 @@
-import math
 from contextlib import ExitStack
 
 import concourse.mybir as mybir
@@ -22,11 +21,8 @@ N = 512
 FLOPS = 2 * 2 * D * Q * T
 
 EXP_CAP = 2.0**60
-SP_CAP = math.log(1.0 + EXP_CAP)
 PIECE = 256
-STORE_WIDTHS = [256, 256, 256, 256]
-ROOT_WIDTHS = [256, 256]
-PICK_WIDTHS = [256, 256]
+STORE_WIDTHS = [128, 128, 256, 256, 256]
 
 
 def spans(widths):
@@ -85,7 +81,7 @@ def tile_attend_agreeingtwo_soft_counts_heads_kernel(tc, query, query2, keys_wor
         nc.vector.tensor_copy(out=dst, in_=src)
         quantize(0)
         dst, src = interleaved(1)
-        nc.scalar.activation(dst, src, ACT.Copy)
+        nc.vector.tensor_copy(out=dst, in_=src)
         quantize(1)
 
         for j in range(2):
@@ -103,54 +99,41 @@ def tile_attend_agreeingtwo_soft_counts_heads_kernel(tc, query, query2, keys_wor
         for j in range(2):
             for h in range(pieces):
                 cols = slice(PIECE * h, PIECE * (h + 1))
-                if j == 0 and h % 2 == 1:
+                if j == 1:
                     nc.vector.tensor_copy(out=score[j][:, cols], in_=banks[j][h][:])
                 else:
                     nc.scalar.activation(score[j][:, cols], banks[j][h][:], ACT.Copy)
 
-        ex = [sb.tile([P, I], F32, name=f"ex{j}") for j in range(2)]
-        picked = [sb.tile([P, I], F32, name=f"picked{j}") for j in range(2)]
-        soft = [sb.tile([P, I], F32, name=f"soft{j}") for j in range(2)]
-        nc.vector.tensor_copy(out=picked[0][:], in_=score[0][:].indirect(offsets[:]))
-        nc.scalar.activation(ex[0][:], picked[0][:], ACT.Exp)
-        for cols in spans(PICK_WIDTHS):
-            nc.vector.tensor_copy(
-                out=picked[1][:, cols], in_=score[1][:].indirect(offsets[:, cols.start // 16 : cols.stop // 16])
-            )
-            nc.scalar.activation(ex[1][:, cols], picked[1][:, cols], ACT.Exp)
-        over_b = sb.tile([P, I], F32, name="over_b")
-        over = sb.tile([P, I], F32, name="over")
-        nc.vector.tensor_scalar_min(ex[0][:], ex[0][:], EXP_CAP)
-        nc.vector.tensor_scalar(over_b[:], picked[1][:], SP_CAP, 1.0 / (SP_CAP * SP_CAP), ALU.max, ALU.mult)
-        nc.vector.tensor_scalar_min(ex[1][:], ex[1][:], EXP_CAP)
-        nc.vector.scalar_tensor_tensor(over[:], picked[0][:], SP_CAP, over_b[:], ALU.max, ALU.mult)
-
-        part = sb.tile([P, I], F32, name="part")
+        ex = sb.tile([P, 2, I], F32, name="ex", tag="ex")
+        capped = sb.tile([P, 2, I], F32, name="capped")
+        logs = [sb.tile([P, I], F32, name=f"logs{j}") for j in range(2)]
+        soft = [sb.tile([P, I], F32, name=f"soft{j}", tag=f"soft{j}") for j in range(2)]
         prod = sb.tile([P, I], F32, name="prod")
-        logu = sb.tile([P, I], F32, name="logu")
         root = sb.tile([P, I], F32, name="root")
         diff = sb.tile([P, I], F32, name="diff")
-        negabs = sb.tile([P, I], F32, name="negabs")
         s = sb.tile([P, I], F32, name="s")
         p = sb.tile([P, I], F32, name="p")
         ws = sb.tile([P, I], F32, name="ws")
         negmax = sb.tile([P, 1], F32, name="negmax")
         total = sb.tile([P, 1], F32, name="total")
         inv = sb.tile([P, 1], F32, name="inv")
-        halves = spans([I // 2, I // 2])
-        for cols in halves:
-            nc.scalar.activation(soft[0][:, cols], ex[0][:, cols], ACT.Ln, bias=1.0)
-            nc.vector.tensor_tensor(part[:, cols], soft[0][:, cols], over[:, cols], ALU.mult)
-        for cols in halves:
-            nc.scalar.activation(soft[1][:, cols], ex[1][:, cols], ACT.Ln, bias=1.0)
-            nc.vector.tensor_tensor(prod[:, cols], part[:, cols], soft[1][:, cols], ALU.mult)
-        for cols in halves:
-            nc.scalar.activation(logu[:, cols], prod[:, cols], ACT.Ln, bias=0.1)
+        for j in range(2):
+            nc.scalar.activation(ex[:, j, :], score[j][:].indirect(offsets[:]), ACT.Exp)
+        picked_a = sb.tile([P, I], F32, name="picked_a")
+        nc.vector.tensor_copy(out=picked_a[:], in_=score[0][:].indirect(offsets[:]))
+        nc.vector.tensor_scalar_min(capped[:], ex[:], EXP_CAP)
+        picked_b = sb.tile([P, I], F32, name="picked_b", tag="ex")
+        nc.vector.tensor_copy(out=picked_b[:], in_=score[1][:].indirect(offsets[:]))
+        picked = [picked_a, picked_b]
         nc.vector.tensor_tensor(diff[:], picked[0][:], picked[1][:], ALU.subtract)
+        for j in range(2):
+            nc.scalar.activation(logs[j][:], capped[:, j, :], ACT.Ln, bias=1.0)
+            nc.vector.tensor_tensor(soft[j][:], logs[j][:], picked[j][:], ALU.max)
+        nc.vector.tensor_tensor(prod[:], soft[0][:], soft[1][:], ALU.mult)
+        negabs = sb.tile([P, I], F32, name="negabs", tag="soft0")
         nc.vector.scalar_tensor_tensor(negabs[:], diff[:], -1.0, diff[:], ALU.mult, ALU.min)
-        for cols in spans(ROOT_WIDTHS):
-            nc.scalar.activation(root[:, cols], logu[:, cols], ACT.Exp, scale=0.5)
-            nc.vector.scalar_tensor_tensor(s[:, cols], root[:, cols], lam_sb[:], negabs[:, cols], ALU.mult, ALU.add)
+        nc.scalar.activation(root[:], prod[:], ACT.Sqrt, bias=0.1)
+        nc.vector.scalar_tensor_tensor(s[:], root[:], lam_sb[:], negabs[:], ALU.mult, ALU.add)
         nc.vector.tensor_reduce(negmax[:], s[:], AX.X, ALU.max, negate=True)
         nc.scalar.activation(p[:], s[:], ACT.Exp, bias=negmax[:], accum_out=total[:])
         nc.vector.reciprocal(inv[:], total[:])

@@ -53,36 +53,38 @@ def tile_attend_agreeingtwo_soft_counts_heads_kernel(tc, query, query2, keys_wor
 
         nc.vector.memset(plane[:].bitcast(U32), 0)
         nc.sync.dma_start(out=raw[0][:], in_=query.rearrange("(p j) w -> p j w", j=PACK))
+        nc.sync.dma_start(out=words[0][:].bitcast(I32), in_=keys_words[0, :, 0:T].bitcast(I32))
         for quad in range(4):
-            nc.scalar.dma_start(
+            nc.sync.dma_start(
                 out=plane[32 * quad : 32 * quad + 4, :].bitcast(I32),
                 in_=keys_scales[0, 4 * quad : 4 * quad + 4, :].bitcast(I32),
             )
         nc.sync.dma_start(out=raw[1][:], in_=query2.rearrange("(p j) w -> p j w", j=PACK))
-        for h in range(2):
-            nc.sync.dma_start(out=words[h][:].bitcast(I32), in_=keys_words[0, :, T * h : T * (h + 1)].bitcast(I32))
+        nc.sync.dma_start(out=words[1][:].bitcast(I32), in_=keys_words[0, :, T : 2 * T].bitcast(I32))
         nc.sync.dma_start(offsets[:], offs)
         nc.sync.dma_start(out=old_sb[:], in_=old)
         nc.sync.dma_start(out=lam_sb[:], in_=lam)
         nc.sync.dma_start(out=fade_sb[:], in_=fade)
         nc.vector.memset(wf[:], 0.0)
 
-        def interleaved(j):
-            dst = grouped[j][:].rearrange("p (c i) t -> p c t i", i=4)
-            src = raw[j][:].rearrange("p t (c i) -> p c t i", i=4)
-            return dst, src
+        def cast(j, cols):
+            dst = grouped[j][:, cols, :].rearrange("p (c i) t -> p c t i", i=4)
+            src = raw[j][:, :, cols].rearrange("p t (c i) -> p c t i", i=4)
+            nc.vector.tensor_copy(out=dst, in_=src)
 
-        def quantize(j):
+        def quantize(j, cols):
             nc.vector.quantize_mx(
-                out=codes[j][:].bitcast(FP8X4), scales=qscale[j][:], in_=grouped[j][:].rearrange("p w t -> p (w t)")
+                out=codes[j][:, cols].bitcast(FP8X4),
+                scales=qscale[j][:, cols],
+                in_=grouped[j][:, cols, :].rearrange("p w t -> p (w t)"),
             )
 
-        dst, src = interleaved(0)
-        nc.vector.tensor_copy(out=dst, in_=src)
-        quantize(0)
-        dst, src = interleaved(1)
-        nc.vector.tensor_copy(out=dst, in_=src)
-        quantize(1)
+        row_halves = spans([Q // 2, Q // 2])
+        for j in range(2):
+            for cols in row_halves:
+                cast(j, cols)
+            for cols in row_halves:
+                quantize(j, cols)
 
         for j in range(2):
             for h in range(pieces):
@@ -104,33 +106,41 @@ def tile_attend_agreeingtwo_soft_counts_heads_kernel(tc, query, query2, keys_wor
                 else:
                     nc.scalar.activation(score[j][:, cols], banks[j][h][:], ACT.Copy)
 
-        ex = sb.tile([P, 2, I], F32, name="ex", tag="ex")
-        capped = sb.tile([P, 2, I], F32, name="capped")
-        logs = [sb.tile([P, I], F32, name=f"logs{j}") for j in range(2)]
-        soft = [sb.tile([P, I], F32, name=f"soft{j}", tag=f"soft{j}") for j in range(2)]
+        H = I // 2
+        slots = [slice(0, H), slice(H, I)]
+        lists = [offsets[:, 0 : H // 16], offsets[:, H // 16 : I // 16]]
+        ex = sb.tile([P, 2, 2, H], F32, name="ex", tag="ex")
+        capped = sb.tile([P, 2, 2, H], F32, name="capped")
+        logs = [sb.tile([P, 2, H], F32, name=f"logs{h}") for h in range(2)]
+        soft = [sb.tile([P, 2, H], F32, name=f"soft{h}", tag=f"soft{h}") for h in range(2)]
         prod = sb.tile([P, I], F32, name="prod")
-        root = sb.tile([P, I], F32, name="root")
         diff = sb.tile([P, I], F32, name="diff")
+        root = sb.tile([P, I], F32, name="root")
         s = sb.tile([P, I], F32, name="s")
         p = sb.tile([P, I], F32, name="p")
         ws = sb.tile([P, I], F32, name="ws")
         negmax = sb.tile([P, 1], F32, name="negmax")
         total = sb.tile([P, 1], F32, name="total")
         inv = sb.tile([P, 1], F32, name="inv")
+        early = sb.tile([P, 2, H], F32, name="early")
         for j in range(2):
-            nc.scalar.activation(ex[:, j, :], score[j][:].indirect(offsets[:]), ACT.Exp)
-        picked_a = sb.tile([P, I], F32, name="picked_a")
-        nc.vector.tensor_copy(out=picked_a[:], in_=score[0][:].indirect(offsets[:]))
+            nc.vector.tensor_copy(out=early[:, j, :], in_=score[j][:].indirect(lists[0]))
+            nc.scalar.activation(ex[:, 1, j, :], score[j][:].indirect(lists[1]), ACT.Exp)
+        for j in range(2):
+            nc.scalar.activation(ex[:, 0, j, :], early[:, j, :], ACT.Exp)
+        nc.vector.tensor_tensor(diff[:, slots[0]], early[:, 0, :], early[:, 1, :], ALU.subtract)
         nc.vector.tensor_scalar_min(capped[:], ex[:], EXP_CAP)
-        picked_b = sb.tile([P, I], F32, name="picked_b", tag="ex")
-        nc.vector.tensor_copy(out=picked_b[:], in_=score[1][:].indirect(offsets[:]))
-        picked = [picked_a, picked_b]
-        nc.vector.tensor_tensor(diff[:], picked[0][:], picked[1][:], ALU.subtract)
+        late = sb.tile([P, 2, H], F32, name="late", tag="ex")
         for j in range(2):
-            nc.scalar.activation(logs[j][:], capped[:, j, :], ACT.Ln, bias=1.0)
-            nc.vector.tensor_tensor(soft[j][:], logs[j][:], picked[j][:], ALU.max)
-        nc.vector.tensor_tensor(prod[:], soft[0][:], soft[1][:], ALU.mult)
-        negabs = sb.tile([P, I], F32, name="negabs", tag="soft0")
+            nc.vector.tensor_copy(out=late[:, j, :], in_=score[j][:].indirect(lists[1]))
+        nc.vector.tensor_tensor(diff[:, slots[1]], late[:, 0, :], late[:, 1, :], ALU.subtract)
+        picked = [early, late]
+        for h in range(2):
+            nc.scalar.activation(logs[h][:], capped[:, h, :, :], ACT.Ln, bias=1.0)
+            nc.vector.tensor_tensor(soft[h][:], logs[h][:], picked[h][:], ALU.max)
+        for h in range(2):
+            nc.vector.tensor_tensor(prod[:, slots[h]], soft[h][:, 0, :], soft[h][:, 1, :], ALU.mult)
+        negabs = sb.tile([P, I], F32, name="negabs", tag="soft1")
         nc.vector.scalar_tensor_tensor(negabs[:], diff[:], -1.0, diff[:], ALU.mult, ALU.min)
         nc.scalar.activation(root[:], prod[:], ACT.Sqrt, bias=0.1)
         nc.vector.scalar_tensor_tensor(s[:], root[:], lam_sb[:], negabs[:], ALU.mult, ALU.add)

from contextlib import ExitStack

import concourse.mybir as mybir

F32 = mybir.dt.float32
BF16 = mybir.dt.bfloat16
I32 = mybir.dt.int32
U32 = mybir.dt.uint32
U16 = mybir.dt.uint16
U8 = mybir.dt.uint8
FP8X4 = mybir.dt.float8_e4m3fn_x4
FP4X4 = mybir.dt.float4_e2m1fn_x4
ALU = mybir.AluOpType
ACT = mybir.ActivationFunctionType
AX = mybir.AxisListType

D, T, I, Q = 512, 1024, 512, 128
P = 128
PACK = 4
N = 512
FLOPS = 2 * 2 * D * Q * T

EXP_CAP = 2.0**60
PIECE = 256
STORE_WIDTHS = [128, 128, 256, 256, 256]


def spans(widths):
    edges = [sum(widths[:j]) for j in range(len(widths) + 1)]
    return [slice(edges[j], edges[j + 1]) for j in range(len(widths))]


def tile_attend_agreeingtwo_soft_counts_heads_kernel(tc, query, query2, keys_words, keys_scales, lam, old, fade, offs, out):
    nc = tc.nc
    with ExitStack() as ctx:
        sb = ctx.enter_context(tc.tile_pool(name="sb", bufs=1))
        ps = ctx.enter_context(tc.psum_pool(name="ps", bufs=1))

        offsets = sb.tile([P, I // 16], U16, name="offsets")
        plane = sb.tile([P, T], U8, name="plane", align_bytes=64)
        words = [sb.tile([P, T], U8, name=f"words{h}", align_bytes=64) for h in range(2)]
        wf = sb.tile([P, T], F32, name="wf")
        old_sb = sb.tile([P, T], F32, name="old_sb")
        lam_sb = sb.tile([P, 1], F32, name="lam_sb")
        fade_sb = sb.tile([P, 1], F32, name="fade_sb")
        raw = [sb.tile([P, PACK, Q], F32, name=f"raw{j}") for j in range(2)]
        grouped = [sb.tile([P, Q, PACK], BF16, name=f"grouped{j}", align_bytes=64) for j in range(2)]
        codes = [sb.tile([P, Q], U32, name=f"codes{j}", align_bytes=64) for j in range(2)]
        qscale = [sb.tile([P, Q], U8, name=f"qscale{j}", align_bytes=64) for j in range(2)]
        score = [sb.tile([P, T], F32, name=f"score{j}") for j in range(2)]
        pieces = T // PIECE
        banks = [[ps.tile([P, PIECE], F32, name=f"bank{j}_{h}") for h in range(pieces)] for j in range(2)]

        nc.vector.memset(plane[:].bitcast(U32), 0)
        nc.sync.dma_start(out=raw[0][:], in_=query.rearrange("(p j) w -> p j w", j=PACK))
        nc.sync.dma_start(out=words[0][:].bitcast(I32), in_=keys_words[0, :, 0:T].bitcast(I32))
        for quad in range(4):
            nc.sync.dma_start(
                out=plane[32 * quad : 32 * quad + 4, :].bitcast(I32),
                in_=keys_scales[0, 4 * quad : 4 * quad + 4, :].bitcast(I32),
            )
        nc.sync.dma_start(out=raw[1][:], in_=query2.rearrange("(p j) w -> p j w", j=PACK))
        nc.sync.dma_start(out=words[1][:].bitcast(I32), in_=keys_words[0, :, T : 2 * T].bitcast(I32))
        nc.sync.dma_start(offsets[:], offs)
        nc.sync.dma_start(out=old_sb[:], in_=old)
        nc.sync.dma_start(out=lam_sb[:], in_=lam)
        nc.sync.dma_start(out=fade_sb[:], in_=fade)
        nc.vector.memset(wf[:], 0.0)

        def cast(j, cols):
            dst = grouped[j][:, cols, :].rearrange("p (c i) t -> p c t i", i=4)
            src = raw[j][:, :, cols].rearrange("p t (c i) -> p c t i", i=4)
            nc.vector.tensor_copy(out=dst, in_=src)

        def quantize(j, cols):
            nc.vector.quantize_mx(
                out=codes[j][:, cols].bitcast(FP8X4),
                scales=qscale[j][:, cols],
                in_=grouped[j][:, cols, :].rearrange("p w t -> p (w t)"),
            )

        row_halves = spans([Q // 2, Q // 2])
        for j in range(2):
            for cols in row_halves:
                cast(j, cols)
            for cols in row_halves:
                quantize(j, cols)

        for j in range(2):
            for h in range(pieces):
                byte0 = 2 * PIECE * h % T
                nc.tensor.matmul_mx(
                    out=banks[j][h][:],
                    lhsT=codes[j][:].bitcast(FP8X4),
                    lhsT_scale=qscale[j][:],
                    rhs=words[2 * PIECE * h // T][:, byte0 : byte0 + 2 * PIECE].bitcast(FP4X4),
                    rhs_scale=plane[:, PIECE * h : PIECE * (h + 1)],
                    start=True,
                    stop=True,
                )
        for j in range(2):
            for h in range(pieces):
                cols = slice(PIECE * h, PIECE * (h + 1))
                if j == 1:
                    nc.vector.tensor_copy(out=score[j][:, cols], in_=banks[j][h][:])
                else:
                    nc.scalar.activation(score[j][:, cols], banks[j][h][:], ACT.Copy)

        H = I // 2
        slots = [slice(0, H), slice(H, I)]
        lists = [offsets[:, 0 : H // 16], offsets[:, H // 16 : I // 16]]
        ex = sb.tile([P, 2, 2, H], F32, name="ex", tag="ex")
        capped = sb.tile([P, 2, 2, H], F32, name="capped")
        logs = [sb.tile([P, 2, H], F32, name=f"logs{h}") for h in range(2)]
        soft = [sb.tile([P, 2, H], F32, name=f"soft{h}", tag=f"soft{h}") for h in range(2)]
        prod = sb.tile([P, I], F32, name="prod")
        diff = sb.tile([P, I], F32, name="diff")
        root = sb.tile([P, I], F32, name="root")
        s = sb.tile([P, I], F32, name="s")
        p = sb.tile([P, I], F32, name="p")
        ws = sb.tile([P, I], F32, name="ws")
        negmax = sb.tile([P, 1], F32, name="negmax")
        total = sb.tile([P, 1], F32, name="total")
        inv = sb.tile([P, 1], F32, name="inv")
        early = sb.tile([P, 2, H], F32, name="early")
        for j in range(2):
            nc.vector.tensor_copy(out=early[:, j, :], in_=score[j][:].indirect(lists[0]))
            nc.scalar.activation(ex[:, 1, j, :], score[j][:].indirect(lists[1]), ACT.Exp)
        for j in range(2):
            nc.scalar.activation(ex[:, 0, j, :], early[:, j, :], ACT.Exp)
        nc.vector.tensor_tensor(diff[:, slots[0]], early[:, 0, :], early[:, 1, :], ALU.subtract)
        nc.vector.tensor_scalar_min(capped[:], ex[:], EXP_CAP)
        late = sb.tile([P, 2, H], F32, name="late", tag="ex")
        for j in range(2):
            nc.vector.tensor_copy(out=late[:, j, :], in_=score[j][:].indirect(lists[1]))
        nc.vector.tensor_tensor(diff[:, slots[1]], late[:, 0, :], late[:, 1, :], ALU.subtract)
        picked = [early, late]
        for h in range(2):
            nc.scalar.activation(logs[h][:], capped[:, h, :, :], ACT.Ln, bias=1.0)
            nc.vector.tensor_tensor(soft[h][:], logs[h][:], picked[h][:], ALU.max)
        for h in range(2):
            nc.vector.tensor_tensor(prod[:, slots[h]], soft[h][:, 0, :], soft[h][:, 1, :], ALU.mult)
        negabs = sb.tile([P, I], F32, name="negabs", tag="soft1")
        nc.vector.scalar_tensor_tensor(negabs[:], diff[:], -1.0, diff[:], ALU.mult, ALU.min)
        nc.scalar.activation(root[:], prod[:], ACT.Sqrt, bias=0.1)
        nc.vector.scalar_tensor_tensor(s[:], root[:], lam_sb[:], negabs[:], ALU.mult, ALU.add)
        nc.vector.tensor_reduce(negmax[:], s[:], AX.X, ALU.max, negate=True)
        nc.scalar.activation(p[:], s[:], ACT.Exp, bias=negmax[:], accum_out=total[:])
        nc.vector.reciprocal(inv[:], total[:])
        nc.vector.tensor_scalar(ws[:], p[:], inv[:], 256.0, ALU.mult, ALU.mult)
        nc.vector.tensor_copy(out=wf[:].indirect(offsets[:]), in_=ws[:])

        for c, cols in enumerate(spans(STORE_WIDTHS)):
            res = sb.tile([P, STORE_WIDTHS[c]], F32, name=f"res{c}")
            nc.vector.scalar_tensor_tensor(res[:], old_sb[:, cols], fade_sb[:], wf[:, cols], ALU.mult, ALU.add)
            nc.sync.dma_start(out=out[:, cols], in_=res[:])
